import numpy as np
import ml_dtypes


def mxq(x, axis, fmt="e4m3"):
    dtype, down = {"e4m3": (ml_dtypes.float8_e4m3fn, 7), "e5m2": (ml_dtypes.float8_e5m2, 14)}[fmt]
    v = np.moveaxis(np.asarray(x, np.float32).astype(ml_dtypes.bfloat16).astype(np.float64), axis, -1)
    blocks = v.reshape(v.shape[:-1] + (-1, 32))
    amax = np.abs(blocks).max(-1, keepdims=True)
    byte = np.maximum(np.where(amax > 0, np.frexp(amax)[1] - 1 + 127, 0) - down, 1)
    scale = np.exp2(byte - 127.0)
    codes = (blocks / scale).astype(np.float32).astype(dtype).astype(np.float64)
    return np.moveaxis((codes * scale).reshape(v.shape), -1, axis)


WIDE = False


def mx_kscale(k):
    if not WIDE:
        return np.ones(k)
    levels = np.array([10, -10, 5, -5, 0])
    if k % 512:
        return np.exp2(np.random.permutation(np.resize(levels, k // 32))).repeat(32)
    a = np.empty((k // 512, 16))
    for p in range(k // 512):
        a[p, :8] = np.random.permutation(np.resize(levels, 8))
        for g in range(8):
            far = levels[np.abs(levels - a[p, g]) >= 10]
            a[p, g + 8] = far[np.random.randint(len(far))]
    return np.exp2(a.ravel()).repeat(32)


def f64(x):
    return np.asarray(x).astype(np.float64)


def striped(idx):
    return np.tile(idx.reshape(-1, 16).T, (8, 1)).astype(np.uint16)


def unstriped(offs):
    return offs[:16].T.reshape(-1).astype(np.int64)


def silu(v):
    return v / (1.0 + np.exp(-np.maximum(v, -700.0)))


K, T, E, C, H, N = 2048, 512, 8, 128, 512, 128


def by_expert(wq, xq):
    return np.concatenate([wq[e].T @ xq[:, e * C:(e + 1) * C] for e in range(E)], axis=1)


def setup_inputs():
    n = np.random.standard_normal
    s = mx_kscale(K)[:, None]
    u = mx_kscale(H)
    first = np.random.permutation(np.repeat(np.arange(E), T // E))
    second = (first + 1 + np.random.permutation(np.repeat(np.arange(E - 1), -(-T // (E - 1)))[:T])) % E
    while np.bincount(second, minlength=E).max() != T // E:
        load = np.bincount(second, minlength=E); hi, lo = int(load.argmax()), int(load.argmin())
        t = np.flatnonzero((second == hi) & (first != lo))[0]; second[t] = lo
    slot_token = np.empty(E * C, np.int64); pos = np.empty((2, T), np.int64); fill = np.zeros(E, np.int64)
    place = np.stack([np.random.permutation(C) for _ in range(E)])
    for r, deal in enumerate((first, second)):
        for t in np.random.permutation(T):
            e = deal[t]; j = e * C + place[e, fill[e]]; fill[e] += 1; slot_token[j] = t; pos[r, t] = j
    g = np.random.uniform(0.2, 0.8, T)
    return {
        "xT": (n((K, T)) * s).astype(np.float32),
        "w1": (n((E, K, H)) / np.sqrt(K) / s[None] * u[None, None, :]).astype(np.float32),
        "w2": (n((E, H, N)) / np.sqrt(H) / u[None, :, None]).astype(np.float32),
        "gate": np.stack([np.tile(g, (N, 1)), np.tile(1.0 - g, (N, 1))]).astype(np.float32),
        "offs": striped(slot_token),
        "pos1": striped(pos[0]),
        "pos2": striped(pos[1]),
    }


def reference(xT, w1, w2, gate, offs, pos1, pos2):
    idx = unstriped(offs)
    xq = mxq(f64(xT)[:, idx], 0, "e4m3")
    h = silu(by_expert(mxq(f64(w1), 1, "e4m3"), xq))
    y = by_expert(mxq(f64(w2), 1, "e4m3"), mxq(h, 0, "e4m3"))
    return f64(gate[0]) * y[:, unstriped(pos1)] + f64(gate[1]) * y[:, unstriped(pos2)]

@@ -1,0 +1,257 @@
+from contextlib import ExitStack
+
+import concourse.mybir as mybir
+
+K, T, E, C, H, N = 2048, 512, 8, 128, 512, 128
+P = 128
+PACK = 4
+K_PASS = P * PACK
+PASSES = K // K_PASS
+PAIR = 2 * C
+FLOPS = 2 * E * C * (K * H + H * N)
+
+F32 = mybir.dt.float32
+BF16 = mybir.dt.bfloat16
+U32 = mybir.dt.uint32
+U16 = mybir.dt.uint16
+U8 = mybir.dt.uint8
+FP8X4 = mybir.dt.float8_e4m3fn_x4
+MULT = mybir.AluOpType.mult
+SILU = mybir.ActivationFunctionType.Silu
+
+SCALAR_QUADS_X = 80
+SCALAR_QUADS_W = 80
+SCALAR_QUADS_LAST = 44
+RAW_BUFS = 6
+
+
+def tile_routed_moe_kernel(tc, xT, w1, w2, gate, offs, pos1, pos2, out):
+    nc = tc.nc
+    x_src = xT.rearrange("(g p j) t -> g p (j t)", p=P, j=PACK)
+    w1_src = w1.rearrange("e (g p j) h -> e p g (j h)", p=P, j=PACK)
+    w2_src = w2.rearrange("e (p j) n -> p e (j n)", j=PACK)
+    gate_src = gate.rearrange("r n t -> n r t")
+
+    with ExitStack() as ctx:
+        keep = ctx.enter_context(tc.tile_pool(name="keep", bufs=1))
+        raws = ctx.enter_context(tc.tile_pool(name="raws", bufs=RAW_BUFS))
+        groups = ctx.enter_context(tc.tile_pool(name="groups", bufs=8))
+        wq = ctx.enter_context(tc.tile_pool(name="wq", bufs=16))
+        slots = ctx.enter_context(tc.tile_pool(name="slots", bufs=2))
+        hid = ctx.enter_context(tc.tile_pool(name="hid", bufs=2))
+        psum_h = ctx.enter_context(tc.psum_pool(name="psum_h", bufs=2))
+        psum_last = ctx.enter_context(tc.psum_pool(name="psum_last", bufs=1))
+        psum_y = ctx.enter_context(tc.psum_pool(name="psum_y", bufs=2))
+
+        offs_t = keep.tile([P, E * C // 16], U16, name="offs_t")
+        pos1_t = keep.tile([P, T // 16], U16, name="pos1_t")
+        pos2_t = keep.tile([P, T // 16], U16, name="pos2_t")
+        x_codes = keep.tile([P, PASSES, T], U32, name="x_codes", align_bytes=64)
+        x_scales = keep.tile([P, T], U8, name="x_scales", align_bytes=64)
+        w2_codes = keep.tile([P, E * N], U32, name="w2_codes", align_bytes=64)
+        w2_scales = keep.tile([P, E * N], U8, name="w2_scales", align_bytes=64)
+        gates = keep.tile([P, 2, T], F32, name="gates")
+        y_all = keep.tile([P, E * C], F32, name="y_all")
+
+        nc.gpsimd.memset(x_scales[:], 0)
+
+        units = []
+        for g in range(PASSES):
+            units.append(("x", 0, g, 1))
+        for e in range(E):
+            if e == E - 1:
+                units += [("w1", e, 0, 2), ("w1", e, 2, 1), ("w1", e, 3, 1)]
+            else:
+                units += [("w1", e, 0, 2), ("w1", e, 2, 2)]
+            if e in (0, 3):
+                units.append(("w2", 0, e // 3, 1))
+
+        loaded = {}
+
+        def load(i):
+            kind, e, g, n = units[i]
+            raw = raws.tile([P, 2, PACK * H], F32, name="raw", align_bytes=64)
+            if kind == "x":
+                nc.sync.dma_start(out=raw[:, 0, :], in_=x_src[g])
+                if g == 0:
+                    nc.sync.dma_start(offs_t[:], offs)
+                    nc.sync.dma_start(pos1_t[:], pos1)
+                    nc.sync.dma_start(pos2_t[:], pos2)
+            elif kind == "w1":
+                if n == 2:
+                    nc.sync.dma_start(out=raw[:], in_=w1_src[e, :, g : g + 2, :])
+                else:
+                    nc.sync.dma_start(out=raw[:, 0, :], in_=w1_src[e, :, g, :])
+            else:
+                nc.sync.dma_start(
+                    out=raw[:, 0, :].rearrange("p (e x) -> p e x", e=4), in_=w2_src[:, 4 * g : 4 * g + 4, :]
+                )
+            loaded[i] = raw
+
+        def spread(dst, src, cut):
+            nc.scalar.copy(dst[:, :cut], src[:, :cut])
+            nc.vector.tensor_copy(dst[:, cut:], src[:, cut:])
+
+        def interleave(kind, e, g, raw, u):
+            grouped = groups.tile([P, PACK * H], BF16, name="grouped", align_bytes=64)
+            if kind == "x":
+                spread(
+                    grouped[:].rearrange("p (c i j) -> p c j i", i=4, j=PACK),
+                    raw[:, u, :].rearrange("p (j c i) -> p c j i", j=PACK, i=4),
+                    SCALAR_QUADS_X,
+                )
+            elif kind == "w1":
+                spread(
+                    grouped[:].rearrange("p (t m j) -> p m j t", t=4, j=PACK),
+                    raw[:, u, :].rearrange("p (j m t) -> p m j t", j=PACK, t=4),
+                    SCALAR_QUADS_LAST if (e, g) == (E - 1, PASSES - 1) else SCALAR_QUADS_W,
+                )
+            else:
+                dst = grouped[:].rearrange("p (e c i j) -> p e c j i", e=4, i=4, j=PACK)
+                src = raw[:, u, :].rearrange("p (e j c i) -> p e c j i", e=4, j=PACK, i=4)
+                for q in range(4):
+                    if q < 2:
+                        nc.scalar.copy(dst[:, q], src[:, q])
+                    else:
+                        nc.vector.tensor_copy(dst[:, q], src[:, q])
+            return grouped
+
+        w1_q = {}
+
+        def quantize(kind, e, g, grouped):
+            if kind == "x":
+                codes, scales = x_codes[:, g, :], x_scales[PACK * g : P, :]
+            elif kind == "w1":
+                wc = wq.tile([P, H], U32, name="wc", align_bytes=64)
+                ws = wq.tile([P, H], U8, name="ws", align_bytes=64)
+                w1_q[e, g] = (wc, ws)
+                codes, scales = wc[:], ws[:]
+            else:
+                codes, scales = w2_codes[:, g * 512 : (g + 1) * 512], w2_scales[:, g * 512 : (g + 1) * 512]
+            nc.vector.quantize_mx(out=codes.bitcast(FP8X4), scales=scales, in_=grouped[:])
+
+        pairs = {}
+
+        def gather(pair, g):
+            if g == 0:
+                pairs[pair] = (
+                    slots.tile([P, PASSES, PAIR], U32, name="slot_codes", align_bytes=64),
+                    slots.tile([P, PAIR], U8, name="slot_scales", align_bytes=64),
+                )
+            sc, ss = pairs[pair]
+            idx = offs_t[:, pair * 16 : (pair + 1) * 16]
+            nc.vector.tensor_copy(sc[:, g, :], x_codes[:, g, :].indirect(idx))
+            if g == PASSES - 1:
+                nc.vector.tensor_copy(ss[:], x_scales[:].indirect(idx))
+
+        h_tiles = {}
+
+        accs = {}
+
+        def multiply1(acc, e, t, g):
+            sc, ss = pairs[e // 2]
+            cols = slice((e % 2) * C, (e % 2 + 1) * C)
+            wc, ws = w1_q[e, g]
+            nc.tensor.matmul_mx(
+                out=acc,
+                lhsT=wc[:, t * P : (t + 1) * P].bitcast(FP8X4),
+                lhsT_scale=ws[:, t * P : (t + 1) * P],
+                rhs=sc[:, g, cols].bitcast(FP8X4),
+                rhs_scale=ss[PACK * g : P, cols],
+                start=(g == 0),
+                stop=(g == PASSES - 1),
+            )
+
+        def layer1(e):
+            acc = psum_h.tile([P, 4, C], F32, name="acc")
+            for t in range(4):
+                for g in range(PASSES):
+                    multiply1(acc[:, t, :], e, t, g)
+            accs[e] = acc
+
+        def activate(e):
+            h = hid.tile([P, C, 4], BF16, name="h", align_bytes=64)
+            nc.scalar.activation(h[:], accs[e][:].rearrange("p t s -> p s t"), SILU)
+            h_tiles[e] = h
+
+        last_accs = [psum_last.tile([P, C], F32, name=f"last{t}") for t in range(4)]
+
+        def activate_last():
+            flat = hid.tile([P, 4, C], BF16, name="flat", align_bytes=64)
+            for t in range(4):
+                nc.scalar.activation(flat[:, t, :], last_accs[t][:], SILU)
+            h = hid.tile([P, C, 4], BF16, name="h", align_bytes=64)
+            nc.vector.tensor_copy(h[:], flat[:].rearrange("p t s -> p s t"))
+            h_tiles[E - 1] = h
+
+        def layer2(e):
+            hc = hid.tile([P, C], U32, name="hc", align_bytes=64)
+            hs = hid.tile([P, C], U8, name="hs", align_bytes=64)
+            nc.vector.quantize_mx(out=hc[:].bitcast(FP8X4), scales=hs[:], in_=h_tiles[e][:].rearrange("p s t -> p (s t)"))
+            acc = psum_y.tile([P, C], F32, name="acc_y")
+            nc.tensor.matmul_mx(
+                out=acc[:],
+                lhsT=w2_codes[:, e * N : (e + 1) * N].bitcast(FP8X4),
+                lhsT_scale=w2_scales[:, e * N : (e + 1) * N],
+                rhs=hc[:].bitcast(FP8X4),
+                rhs_scale=hs[:],
+                start=True,
+                stop=True,
+            )
+            nc.scalar.copy(y_all[:, e * C : (e + 1) * C], acc[:])
+
+        chunks = []
+        for i, (kind, e, g, n) in enumerate(units):
+            for u in range(n):
+                chunks.append((kind, e, g + u, i, u))
+
+        ahead = RAW_BUFS - 1
+        for i in range(ahead):
+            load(i)
+
+        def finish(chunk):
+            kind, e, g, grouped = chunk
+            quantize(kind, e, g, grouped)
+            if kind == "x":
+                gather(0, g)
+            if kind == "w1":
+                pair = e // 2 + 1
+                if pair < E // 2 and g >= 2:
+                    gather(pair, (e % 2) * 2 + g - 2)
+                if e == E - 1:
+                    for t in range(4):
+                        multiply1(last_accs[t][:], e, t, g)
+                elif g == PASSES - 1:
+                    layer1(e)
+
+        pending = None
+        to_activate = []
+        to_layer2 = []
+        for kind, e, g, i, u in chunks:
+            if u == 0:
+                if i + ahead < len(units):
+                    load(i + ahead)
+                elif i + ahead == len(units):
+                    nc.sync.dma_start(out=gates[:], in_=gate_src)
+            grouped = interleave(kind, e, g, loaded[i], u)
+            if pending is not None:
+                finish(pending)
+            while to_layer2:
+                layer2(to_layer2.pop(0))
+            while to_activate:
+                activate(to_activate[0])
+                to_layer2.append(to_activate.pop(0))
+            if pending is not None and pending[0] == "w1" and pending[2] == PASSES - 1:
+                to_activate.append(pending[1])
+            pending = (kind, e, g, grouped)
+        finish(pending)
+        activate_last()
+        layer2(E - 1)
+
+        first = keep.tile([P, T], F32, name="first")
+        second = keep.tile([P, T], F32, name="second")
+        total = keep.tile([P, T], F32, name="total")
+        nc.vector.tensor_tensor(first[:], y_all[:].indirect(pos1_t[:]), gates[:, 0, :], MULT)
+        nc.vector.tensor_tensor(second[:], y_all[:].indirect(pos2_t[:]), gates[:, 1, :], MULT)
+        nc.vector.tensor_add(total[:], first[:], second[:])
+        nc.sync.dma_start(out=out, in_=total[:])

@@ -20,7 +20,7 @@ MULT = mybir.AluOpType.mult
 SILU = mybir.ActivationFunctionType.Silu
 
 SCALAR_QUADS_X = 80
-SCALAR_QUADS_W = 80
+SCALAR_QUADS_W = 72
 SCALAR_QUADS_LAST = 44
 RAW_BUFS = 6
 
@@ -35,8 +35,8 @@ def tile_routed_moe_kernel(tc, xT, w1, w2, gate, offs, pos1, pos2, out):
     with ExitStack() as ctx:
         keep = ctx.enter_context(tc.tile_pool(name="keep", bufs=1))
         raws = ctx.enter_context(tc.tile_pool(name="raws", bufs=RAW_BUFS))
-        groups = ctx.enter_context(tc.tile_pool(name="groups", bufs=8))
-        wq = ctx.enter_context(tc.tile_pool(name="wq", bufs=16))
+        groups = ctx.enter_context(tc.tile_pool(name="groups", bufs=4))
+        wq = ctx.enter_context(tc.tile_pool(name="wq", bufs=8))
         slots = ctx.enter_context(tc.tile_pool(name="slots", bufs=2))
         hid = ctx.enter_context(tc.tile_pool(name="hid", bufs=2))
         psum_h = ctx.enter_context(tc.psum_pool(name="psum_h", bufs=2))
@@ -92,43 +92,48 @@ def tile_routed_moe_kernel(tc, xT, w1, w2, gate, offs, pos1, pos2, out):
             nc.scalar.copy(dst[:, :cut], src[:, :cut])
             nc.vector.tensor_copy(dst[:, cut:], src[:, cut:])
 
-        def interleave(kind, e, g, raw, u):
-            grouped = groups.tile([P, PACK * H], BF16, name="grouped", align_bytes=64)
+        def interleave(kind, e, g, raw, n):
+            grouped = groups.tile([P, 2, PACK * H], BF16, name="grouped", align_bytes=64)
             if kind == "x":
                 spread(
-                    grouped[:].rearrange("p (c i j) -> p c j i", i=4, j=PACK),
-                    raw[:, u, :].rearrange("p (j c i) -> p c j i", j=PACK, i=4),
+                    grouped[:, 0, :].rearrange("p (c i j) -> p c j i", i=4, j=PACK),
+                    raw[:, 0, :].rearrange("p (j c i) -> p c j i", j=PACK, i=4),
                     SCALAR_QUADS_X,
                 )
+            elif kind == "w1" and n == 2:
+                dst = grouped[:].rearrange("p u (t m j) -> p u m j t", t=4, j=PACK)
+                src = raw[:].rearrange("p u (j m t) -> p u m j t", j=PACK, t=4)
+                cut = SCALAR_QUADS_W
+                nc.scalar.copy(dst[:, :, :cut], src[:, :, :cut])
+                nc.vector.tensor_copy(dst[:, :, cut:], src[:, :, cut:])
             elif kind == "w1":
                 spread(
-                    grouped[:].rearrange("p (t m j) -> p m j t", t=4, j=PACK),
-                    raw[:, u, :].rearrange("p (j m t) -> p m j t", j=PACK, t=4),
-                    SCALAR_QUADS_LAST if (e, g) == (E - 1, PASSES - 1) else SCALAR_QUADS_W,
+                    grouped[:, 0, :].rearrange("p (t m j) -> p m j t", t=4, j=PACK),
+                    raw[:, 0, :].rearrange("p (j m t) -> p m j t", j=PACK, t=4),
+                    SCALAR_QUADS_LAST,
                 )
             else:
-                dst = grouped[:].rearrange("p (e c i j) -> p e c j i", e=4, i=4, j=PACK)
-                src = raw[:, u, :].rearrange("p (e j c i) -> p e c j i", e=4, j=PACK, i=4)
-                for q in range(4):
-                    if q < 2:
-                        nc.scalar.copy(dst[:, q], src[:, q])
-                    else:
-                        nc.vector.tensor_copy(dst[:, q], src[:, q])
+                dst = grouped[:, 0, :].rearrange("p (e c i j) -> p e c j i", e=4, i=4, j=PACK)
+                src = raw[:, 0, :].rearrange("p (e j c i) -> p e c j i", e=4, j=PACK, i=4)
+                nc.scalar.copy(dst[:, :2], src[:, :2])
+                nc.vector.tensor_copy(dst[:, 2:], src[:, 2:])
             return grouped
 
         w1_q = {}
 
-        def quantize(kind, e, g, grouped):
+        def quantize(kind, e, g, n, grouped):
             if kind == "x":
                 codes, scales = x_codes[:, g, :], x_scales[PACK * g : P, :]
             elif kind == "w1":
-                wc = wq.tile([P, H], U32, name="wc", align_bytes=64)
-                ws = wq.tile([P, H], U8, name="ws", align_bytes=64)
-                w1_q[e, g] = (wc, ws)
-                codes, scales = wc[:], ws[:]
+                wc = wq.tile([P, 2 * H], U32, name="wc", align_bytes=64)
+                ws = wq.tile([P, 2 * H], U8, name="ws", align_bytes=64)
+                for u in range(n):
+                    w1_q[e, g + u] = (wc, ws, u * H)
+                codes, scales = wc[:, : n * H], ws[:, : n * H]
             else:
                 codes, scales = w2_codes[:, g * 512 : (g + 1) * 512], w2_scales[:, g * 512 : (g + 1) * 512]
-            nc.vector.quantize_mx(out=codes.bitcast(FP8X4), scales=scales, in_=grouped[:])
+            source = grouped[:].rearrange("p u x -> p (u x)") if n == 2 else grouped[:, 0, :]
+            nc.vector.quantize_mx(out=codes.bitcast(FP8X4), scales=scales, in_=source)
 
         pairs = {}
 
@@ -151,11 +156,11 @@ def tile_routed_moe_kernel(tc, xT, w1, w2, gate, offs, pos1, pos2, out):
         def multiply1(acc, e, t, g):
             sc, ss = pairs[e // 2]
             cols = slice((e % 2) * C, (e % 2 + 1) * C)
-            wc, ws = w1_q[e, g]
+            wc, ws, base = w1_q[e, g]
             nc.tensor.matmul_mx(
                 out=acc,
-                lhsT=wc[:, t * P : (t + 1) * P].bitcast(FP8X4),
-                lhsT_scale=ws[:, t * P : (t + 1) * P],
+                lhsT=wc[:, base + t * P : base + (t + 1) * P].bitcast(FP8X4),
+                lhsT_scale=ws[:, base + t * P : base + (t + 1) * P],
                 rhs=sc[:, g, cols].bitcast(FP8X4),
                 rhs_scale=ss[PACK * g : P, cols],
                 start=(g == 0),
@@ -184,13 +189,17 @@ def tile_routed_moe_kernel(tc, xT, w1, w2, gate, offs, pos1, pos2, out):
             nc.vector.tensor_copy(h[:], flat[:].rearrange("p t s -> p s t"))
             h_tiles[E - 1] = h
 
+        y_accs = {}
+
         def layer2(e):
             hc = hid.tile([P, C], U32, name="hc", align_bytes=64)
             hs = hid.tile([P, C], U8, name="hs", align_bytes=64)
             nc.vector.quantize_mx(out=hc[:].bitcast(FP8X4), scales=hs[:], in_=h_tiles[e][:].rearrange("p s t -> p (s t)"))
-            acc = psum_y.tile([P, C], F32, name="acc_y")
+            if e % 2 == 0:
+                y_accs[e // 2] = psum_y.tile([P, PAIR], F32, name="acc_y")
+            acc = y_accs[e // 2]
             nc.tensor.matmul_mx(
-                out=acc[:],
+                out=acc[:, (e % 2) * C : (e % 2 + 1) * C],
                 lhsT=w2_codes[:, e * N : (e + 1) * N].bitcast(FP8X4),
                 lhsT_scale=w2_scales[:, e * N : (e + 1) * N],
                 rhs=hc[:].bitcast(FP8X4),
@@ -198,42 +207,39 @@ def tile_routed_moe_kernel(tc, xT, w1, w2, gate, offs, pos1, pos2, out):
                 start=True,
                 stop=True,
             )
-            nc.scalar.copy(y_all[:, e * C : (e + 1) * C], acc[:])
-
-        chunks = []
-        for i, (kind, e, g, n) in enumerate(units):
-            for u in range(n):
-                chunks.append((kind, e, g + u, i, u))
+            if e % 2 == 1:
+                nc.scalar.copy(y_all[:, (e - 1) * C : (e + 1) * C], acc[:])
 
         ahead = RAW_BUFS - 1
         for i in range(ahead):
             load(i)
 
         def finish(chunk):
-            kind, e, g, grouped = chunk
-            quantize(kind, e, g, grouped)
+            kind, e, g, n, grouped = chunk
+            quantize(kind, e, g, n, grouped)
             if kind == "x":
                 gather(0, g)
             if kind == "w1":
                 pair = e // 2 + 1
-                if pair < E // 2 and g >= 2:
-                    gather(pair, (e % 2) * 2 + g - 2)
+                if pair < E // 2 and g == 2:
+                    gather(pair, (e % 2) * 2)
+                    gather(pair, (e % 2) * 2 + 1)
                 if e == E - 1:
-                    for t in range(4):
-                        multiply1(last_accs[t][:], e, t, g)
-                elif g == PASSES - 1:
+                    for u in range(n):
+                        for t in range(4):
+                            multiply1(last_accs[t][:], e, t, g + u)
+                elif g + n == PASSES:
                     layer1(e)
 
         pending = None
         to_activate = []
         to_layer2 = []
-        for kind, e, g, i, u in chunks:
-            if u == 0:
-                if i + ahead < len(units):
-                    load(i + ahead)
-                elif i + ahead == len(units):
-                    nc.sync.dma_start(out=gates[:], in_=gate_src)
-            grouped = interleave(kind, e, g, loaded[i], u)
+        for i, (kind, e, g, n) in enumerate(units):
+            if i + ahead < len(units):
+                load(i + ahead)
+            elif i + ahead == len(units):
+                nc.sync.dma_start(out=gates[:], in_=gate_src)
+            grouped = interleave(kind, e, g, loaded[i], n)
             if pending is not None:
                 finish(pending)
             while to_layer2:
@@ -241,9 +247,9 @@ def tile_routed_moe_kernel(tc, xT, w1, w2, gate, offs, pos1, pos2, out):
             while to_activate:
                 activate(to_activate[0])
                 to_layer2.append(to_activate.pop(0))
-            if pending is not None and pending[0] == "w1" and pending[2] == PASSES - 1:
+            if pending is not None and pending[0] == "w1" and pending[2] + pending[3] == PASSES:
                 to_activate.append(pending[1])
-            pending = (kind, e, g, grouped)
+            pending = (kind, e, g, n, grouped)
         finish(pending)
         activate_last()
         layer2(E - 1)

from contextlib import ExitStack

import concourse.mybir as mybir

K, T, E, C, H, N = 2048, 512, 8, 128, 512, 128
P = 128
PACK = 4
K_PASS = P * PACK
PASSES = K // K_PASS
PAIR = 2 * C
FLOPS = 2 * E * C * (K * H + H * N)

F32 = mybir.dt.float32
BF16 = mybir.dt.bfloat16
U32 = mybir.dt.uint32
U16 = mybir.dt.uint16
U8 = mybir.dt.uint8
FP8X4 = mybir.dt.float8_e4m3fn_x4
MULT = mybir.AluOpType.mult
SILU = mybir.ActivationFunctionType.Silu

SCALAR_QUADS_X = 80
SCALAR_QUADS_W = 72
SCALAR_QUADS_LAST = 44
RAW_BUFS = 6


def tile_routed_moe_kernel(tc, xT, w1, w2, gate, offs, pos1, pos2, out):
    nc = tc.nc
    x_src = xT.rearrange("(g p j) t -> g p (j t)", p=P, j=PACK)
    w1_src = w1.rearrange("e (g p j) h -> e p g (j h)", p=P, j=PACK)
    w2_src = w2.rearrange("e (p j) n -> p e (j n)", j=PACK)
    gate_src = gate.rearrange("r n t -> n r t")

    with ExitStack() as ctx:
        keep = ctx.enter_context(tc.tile_pool(name="keep", bufs=1))
        raws = ctx.enter_context(tc.tile_pool(name="raws", bufs=RAW_BUFS))
        groups = ctx.enter_context(tc.tile_pool(name="groups", bufs=4))
        wq = ctx.enter_context(tc.tile_pool(name="wq", bufs=8))
        slots = ctx.enter_context(tc.tile_pool(name="slots", bufs=2))
        hid = ctx.enter_context(tc.tile_pool(name="hid", bufs=2))
        psum_h = ctx.enter_context(tc.psum_pool(name="psum_h", bufs=2))
        psum_last = ctx.enter_context(tc.psum_pool(name="psum_last", bufs=1))
        psum_y = ctx.enter_context(tc.psum_pool(name="psum_y", bufs=2))

        offs_t = keep.tile([P, E * C // 16], U16, name="offs_t")
        pos1_t = keep.tile([P, T // 16], U16, name="pos1_t")
        pos2_t = keep.tile([P, T // 16], U16, name="pos2_t")
        x_codes = keep.tile([P, PASSES, T], U32, name="x_codes", align_bytes=64)
        x_scales = keep.tile([P, T], U8, name="x_scales", align_bytes=64)
        w2_codes = keep.tile([P, E * N], U32, name="w2_codes", align_bytes=64)
        w2_scales = keep.tile([P, E * N], U8, name="w2_scales", align_bytes=64)
        gates = keep.tile([P, 2, T], F32, name="gates")
        y_all = keep.tile([P, E * C], F32, name="y_all")

        nc.gpsimd.memset(x_scales[:], 0)

        units = []
        for g in range(PASSES):
            units.append(("x", 0, g, 1))
        for e in range(E):
            if e == E - 1:
                units += [("w1", e, 0, 2), ("w1", e, 2, 1), ("w1", e, 3, 1)]
            else:
                units += [("w1", e, 0, 2), ("w1", e, 2, 2)]
            if e in (0, 3):
                units.append(("w2", 0, e // 3, 1))

        loaded = {}

        def load(i):
            kind, e, g, n = units[i]
            raw = raws.tile([P, 2, PACK * H], F32, name="raw", align_bytes=64)
            if kind == "x":
                nc.sync.dma_start(out=raw[:, 0, :], in_=x_src[g])
                if g == 0:
                    nc.sync.dma_start(offs_t[:], offs)
                    nc.sync.dma_start(pos1_t[:], pos1)
                    nc.sync.dma_start(pos2_t[:], pos2)
            elif kind == "w1":
                if n == 2:
                    nc.sync.dma_start(out=raw[:], in_=w1_src[e, :, g : g + 2, :])
                else:
                    nc.sync.dma_start(out=raw[:, 0, :], in_=w1_src[e, :, g, :])
            else:
                nc.sync.dma_start(
                    out=raw[:, 0, :].rearrange("p (e x) -> p e x", e=4), in_=w2_src[:, 4 * g : 4 * g + 4, :]
                )
            loaded[i] = raw

        def spread(dst, src, cut):
            nc.scalar.copy(dst[:, :cut], src[:, :cut])
            nc.vector.tensor_copy(dst[:, cut:], src[:, cut:])

        def interleave(kind, e, g, raw, n):
            grouped = groups.tile([P, 2, PACK * H], BF16, name="grouped", align_bytes=64)
            if kind == "x":
                spread(
                    grouped[:, 0, :].rearrange("p (c i j) -> p c j i", i=4, j=PACK),
                    raw[:, 0, :].rearrange("p (j c i) -> p c j i", j=PACK, i=4),
                    SCALAR_QUADS_X,
                )
            elif kind == "w1" and n == 2:
                dst = grouped[:].rearrange("p u (t m j) -> p u m j t", t=4, j=PACK)
                src = raw[:].rearrange("p u (j m t) -> p u m j t", j=PACK, t=4)
                cut = SCALAR_QUADS_W
                nc.scalar.copy(dst[:, :, :cut], src[:, :, :cut])
                nc.vector.tensor_copy(dst[:, :, cut:], src[:, :, cut:])
            elif kind == "w1":
                spread(
                    grouped[:, 0, :].rearrange("p (t m j) -> p m j t", t=4, j=PACK),
                    raw[:, 0, :].rearrange("p (j m t) -> p m j t", j=PACK, t=4),
                    SCALAR_QUADS_LAST,
                )
            else:
                dst = grouped[:, 0, :].rearrange("p (e c i j) -> p e c j i", e=4, i=4, j=PACK)
                src = raw[:, 0, :].rearrange("p (e j c i) -> p e c j i", e=4, j=PACK, i=4)
                nc.scalar.copy(dst[:, :2], src[:, :2])
                nc.vector.tensor_copy(dst[:, 2:], src[:, 2:])
            return grouped

        w1_q = {}

        def quantize(kind, e, g, n, grouped):
            if kind == "x":
                codes, scales = x_codes[:, g, :], x_scales[PACK * g : P, :]
            elif kind == "w1":
                wc = wq.tile([P, 2 * H], U32, name="wc", align_bytes=64)
                ws = wq.tile([P, 2 * H], U8, name="ws", align_bytes=64)
                for u in range(n):
                    w1_q[e, g + u] = (wc, ws, u * H)
                codes, scales = wc[:, : n * H], ws[:, : n * H]
            else:
                codes, scales = w2_codes[:, g * 512 : (g + 1) * 512], w2_scales[:, g * 512 : (g + 1) * 512]
            source = grouped[:].rearrange("p u x -> p (u x)") if n == 2 else grouped[:, 0, :]
            nc.vector.quantize_mx(out=codes.bitcast(FP8X4), scales=scales, in_=source)

        pairs = {}

        def gather(pair, g):
            if g == 0:
                pairs[pair] = (
                    slots.tile([P, PASSES, PAIR], U32, name="slot_codes", align_bytes=64),
                    slots.tile([P, PAIR], U8, name="slot_scales", align_bytes=64),
                )
            sc, ss = pairs[pair]
            idx = offs_t[:, pair * 16 : (pair + 1) * 16]
            nc.vector.tensor_copy(sc[:, g, :], x_codes[:, g, :].indirect(idx))
            if g == PASSES - 1:
                nc.vector.tensor_copy(ss[:], x_scales[:].indirect(idx))

        h_tiles = {}

        accs = {}

        def multiply1(acc, e, t, g):
            sc, ss = pairs[e // 2]
            cols = slice((e % 2) * C, (e % 2 + 1) * C)
            wc, ws, base = w1_q[e, g]
            nc.tensor.matmul_mx(
                out=acc,
                lhsT=wc[:, base + t * P : base + (t + 1) * P].bitcast(FP8X4),
                lhsT_scale=ws[:, base + t * P : base + (t + 1) * P],
                rhs=sc[:, g, cols].bitcast(FP8X4),
                rhs_scale=ss[PACK * g : P, cols],
                start=(g == 0),
                stop=(g == PASSES - 1),
            )

        def layer1(e):
            acc = psum_h.tile([P, 4, C], F32, name="acc")
            for t in range(4):
                for g in range(PASSES):
                    multiply1(acc[:, t, :], e, t, g)
            accs[e] = acc

        def activate(e):
            h = hid.tile([P, C, 4], BF16, name="h", align_bytes=64)
            nc.scalar.activation(h[:], accs[e][:].rearrange("p t s -> p s t"), SILU)
            h_tiles[e] = h

        last_accs = [psum_last.tile([P, C], F32, name=f"last{t}") for t in range(4)]

        def activate_last():
            flat = hid.tile([P, 4, C], BF16, name="flat", align_bytes=64)
            for t in range(4):
                nc.scalar.activation(flat[:, t, :], last_accs[t][:], SILU)
            h = hid.tile([P, C, 4], BF16, name="h", align_bytes=64)
            nc.vector.tensor_copy(h[:], flat[:].rearrange("p t s -> p s t"))
            h_tiles[E - 1] = h

        y_accs = {}

        def layer2(e):
            hc = hid.tile([P, C], U32, name="hc", align_bytes=64)
            hs = hid.tile([P, C], U8, name="hs", align_bytes=64)
            nc.vector.quantize_mx(out=hc[:].bitcast(FP8X4), scales=hs[:], in_=h_tiles[e][:].rearrange("p s t -> p (s t)"))
            if e % 2 == 0:
                y_accs[e // 2] = psum_y.tile([P, PAIR], F32, name="acc_y")
            acc = y_accs[e // 2]
            nc.tensor.matmul_mx(
                out=acc[:, (e % 2) * C : (e % 2 + 1) * C],
                lhsT=w2_codes[:, e * N : (e + 1) * N].bitcast(FP8X4),
                lhsT_scale=w2_scales[:, e * N : (e + 1) * N],
                rhs=hc[:].bitcast(FP8X4),
                rhs_scale=hs[:],
                start=True,
                stop=True,
            )
            if e % 2 == 1:
                nc.scalar.copy(y_all[:, (e - 1) * C : (e + 1) * C], acc[:])

        ahead = RAW_BUFS - 1
        for i in range(ahead):
            load(i)

        def finish(chunk):
            kind, e, g, n, grouped = chunk
            quantize(kind, e, g, n, grouped)
            if kind == "x":
                gather(0, g)
            if kind == "w1":
                pair = e // 2 + 1
                if pair < E // 2 and g == 2:
                    gather(pair, (e % 2) * 2)
                    gather(pair, (e % 2) * 2 + 1)
                if e == E - 1:
                    for u in range(n):
                        for t in range(4):
                            multiply1(last_accs[t][:], e, t, g + u)
                elif g + n == PASSES:
                    layer1(e)

        pending = None
        to_activate = []
        to_layer2 = []
        for i, (kind, e, g, n) in enumerate(units):
            if i + ahead < len(units):
                load(i + ahead)
            elif i + ahead == len(units):
                nc.sync.dma_start(out=gates[:], in_=gate_src)
            grouped = interleave(kind, e, g, loaded[i], n)
            if pending is not None:
                finish(pending)
            while to_layer2:
                layer2(to_layer2.pop(0))
            while to_activate:
                activate(to_activate[0])
                to_layer2.append(to_activate.pop(0))
            if pending is not None and pending[0] == "w1" and pending[2] + pending[3] == PASSES:
                to_activate.append(pending[1])
            pending = (kind, e, g, n, grouped)
        finish(pending)
        activate_last()
        layer2(E - 1)

        first = keep.tile([P, T], F32, name="first")
        second = keep.tile([P, T], F32, name="second")
        total = keep.tile([P, T], F32, name="total")
        nc.vector.tensor_tensor(first[:], y_all[:].indirect(pos1_t[:]), gates[:, 0, :], MULT)
        nc.vector.tensor_tensor(second[:], y_all[:].indirect(pos2_t[:]), gates[:, 1, :], MULT)
        nc.vector.tensor_add(total[:], first[:], second[:])
        nc.sync.dma_start(out=out, in_=total[:])
